import numpy as np, ml_dtypes
CORES = [21,109,149,237,277,365,405,493,150,406]
N = 10
import mx_ref
KO = 2
F = np.float32(1.3)
OWN = [2,9,2,2,9,2,9,2,9,9]
BF = ml_dtypes.bfloat16
def tile(rs):
    return np.stack(rs, axis=2).reshape(128, -1).astype(BF)
def pick(b):
    s = np.zeros((128, 128, 4), np.float32)
    s[np.arange(128), np.arange(128), b] = 1.0
    return mx_ref.quantize(s.reshape(128, 512).astype(BF))
def pk(c, s, i=0):
    return (np.ascontiguousarray(c[:, 512 * i:512 * i + 512]), mx_ref.live(s[:, 128 * i:128 * i + 128]))
def inputs(rng, e, E):
    def f(*shape):
        v = (rng.standard_normal(shape, dtype=np.float32) * np.exp2(rng.integers(-2, 3, shape[:-1] + (1,)))).astype(BF)
        return mx_ref.spread((v.astype(np.float32) * np.exp2(rng.integers(-E, E + 1, shape[:-2] + (1, 1))).astype(np.float32)).astype(BF), rng, e)
    def packed(k):
        c = np.zeros((N, 128, k * 512), np.uint8); s = np.zeros((N, 128, k * 128), np.uint8)
        for r in range(N):
            for i in range(k):
                a, b = mx_ref.quantize(f(128, 512)); c[r][:, 512 * i:512 * i + 512] = a; s[r][:, 128 * i:128 * i + 128] = mx_ref.plane(b, rng)
        return c, s
    d = {}
    d["kc"], d["ks"] = packed(KO)
    d["q"] = f(N, 128, 512)
    return d
def setup_inputs(rng):
    return inputs(rng, 0, 0)
def setup_inputs_blocks(rng):
    return inputs(rng, 4, 0)
def setup_inputs_wide(rng):
    return inputs(rng, 0, 8)
def reference(kc, ks, q):
    S = [pick(t) for t in range(4)]
    anew = lambda p, i: mx_ref.quantize(tile([mx_ref.matmul(S[t], pk(kc[p], ks[p], i)) * F for t in range(4)]))
    y = np.full((N, 128, 1280), np.nan, np.float32)
    for o in range(N):
        if OWN[o] != o: continue
        qq = mx_ref.quantize(q[o])
        M = [pk(kc[o], ks[o], i) for i in range(KO)] + [anew(p, i) for p in range(N) if p != o and OWN[p] == o for i in range(KO)]
        y[o][:, :128 * len(M)] = np.concatenate([mx_ref.matmul(qq, m) for m in M], axis=1)
    return {"y": y}

import numpy as np
from concourse.bass import DstId, RemoteDMATransfer
from concourse.mybir import dt, AluOpType, ActivationFunctionType

U8 = dt.uint8
W = 128
KO = 2
FACTOR = float(np.float32(1.3))

SCRATCH = {
    "mc": ("sbuf", [128, 1280], "float8_e4m3fn_x4"),
    "ms": ("sbuf", [128, 1280], "uint8"),
    "one": ("sbuf", [128, 128], "bfloat16"),
    "z": ("sbuf", [128, 516], "bfloat16"),
    "sc": ("sbuf", [128, 512], "float8_e4m3fn_x4"),
    "ss": ("sbuf", [128, 512], "uint8"),
    "h": ("sbuf", [128, 1024], "bfloat16"),
    "kq": ("sbuf", [128, 256], "float8_e4m3fn_x4"),
    "kqs": ("sbuf", [128, 256], "uint8"),
    "rc": ("sbuf", [128, 256], "float8_e4m3fn_x4"),
    "rp": ("sbuf", [128, 256], "uint8"),
    "qb": ("sbuf", [128, 512], "bfloat16"),
    "qc": ("sbuf", [128, 128], "float8_e4m3fn_x4"),
    "qs": ("sbuf", [128, 128], "uint8"),
    "yo": ("sbuf", [128, 1280], "float32"),
    "ps": ("psum", [128, 4096], "float32"),
}
SEMAPHORES = (["ld", "lq", "ms0", "af", "sq", "qd0", "qd1", "hh0", "hh1", "qq", "sent", "st"]
              + ["r%d" % k for k in range(4)] + ["mm%d" % k for k in range(8)] + ["arr%d" % k for k in range(4)]
              + ["mo%d" % k for k in range(8)] + ["cp%d" % k for k in range(5)])

BOTH = ("qd0", "qd1")
PLANE0 = (("qd0",), [("p", 0, W, 0, 0, 2)])
CODES = ((), [("c", 0, W, 0, 0, 2), ("c", W, 2 * W, 1, 1, 2)])
TWO = [PLANE0, (("qd1",), [("p", W, 2 * W, 1, 1, 2)]), CODES]
CHIP = [PLANE0, (("qd1",), [("p", W, 2 * W, 1, 0, 2)]), CODES]
PLAN = {"direct": [(BOTH, [("c", 0, 2 * W, 0, 0, 1)]), ((), [("p", 0, 2 * W, 0, 0, 1)])],
        "chip": CHIP, "rank": TWO, "far": TWO}
_CACHE = {}


def engines(mask, part, of):
    bits = [b for b in range(16) if mask >> b & 1]
    return sum(1 << b for b in bits[part::of])


def count(mask):
    return bin(mask).count("1")


def roads(T, topo):
    if _CACHE:
        return _CACHE
    cores, own = T.cores, T.tables["OWN"]
    every = range(512)
    calls, taken, seen = {}, set(cores), {}

    def at(x):
        return (topo.host(x), topo.chip(x))

    def other_rack(a, b):
        return topo.rack(topo.host(a)) != topo.rack(topo.host(b))

    def pick(cands, near):
        c = sorted((x for x in cands if x not in taken), key=lambda x: (topo.die(x) != near, x))[0]
        taken.add(c)
        return c

    def say(core, waits, tr):
        calls.setdefault(core, []).append((waits, tr))

    first, second = [], []
    for p in range(len(cores)):
        if own[p] != p:
            (first if topo.may_write(cores[p], cores[own[p]]) else second).append(p)
    for p in first:
        src, dst = cores[p], cores[own[p]]
        for waits, call in PLAN["direct"]:
            say(src, [(w, 1) for w in waits], [((k, a, b, None), p, dst, engines(topo.mask(src, dst), part, of), True)
                                               for k, a, b, _, part, of in call])
    for p in second:
        src, dst = cores[p], cores[own[p]]
        d = topo.die(src)
        two = [x for x in every if x != src and topo.may_write(src, x) and topo.may_write(x, dst)]
        chip = [x for x in two if at(x) == at(src)]
        ranks = [x for x in two if x in cores and topo.chip(x) == topo.chip(dst)]
        if chip:
            kind, X = "chip", [pick(chip, 1 - d), pick(chip, d)]
        elif ranks:
            kind, X = "rank", [[x for x in ranks if other_rack(x, src)][0], [x for x in ranks if not other_rack(x, src)][0]]
        else:
            far = [x for x in two if other_rack(x, src) and topo.chip(x) == topo.chip(src)]
            near = [x for x in two if topo.same_plane(src, x) and topo.host(x) != topo.host(src)
                    and any(topo.mates(x, z) and topo.chip(z) == topo.chip(dst) for z in every)]
            kind, X = "far", [pick(far, d), pick(near, d)]
        for waits, call in PLAN[kind]:
            tr = []
            for k, a, b, to, part, of in call:
                x = X[to]
                n = seen.get(x, 0)
                seen[x] = n + 1
                tr.append(((k, a, b, "r%d" % n), p, x, engines(topo.mask(src, x), part, of), False))
            say(src, [(w, 1) for w in waits], tr)
            for piece, _, x, m, _f in tr:
                say(x, [(piece[3], count(m))], [(piece, p, dst, topo.mask(x, dst), True)])
    slot = {}
    for o in range(len(cores)):
        mine = [p for p in range(len(cores)) if own[o] == o and own[p] == o and p != o]
        for k, p in enumerate(mine):
            slot[p] = k
    need = {p: 0 for p in slot}
    for c in calls:
        for _, tr in calls[c]:
            for piece, p, dst, m, final in tr:
                if final:
                    need[p] += count(m)
    _CACHE["calls"] = calls
    _CACHE["slot"] = slot
    _CACHE["need"] = need
    _CACHE["second"] = second
    return _CACHE


def remote(g, core, T, topo, R):
    sent = 0
    for waits, tr in R["calls"].get(core, []):
        for s, v in waits:
            g.wait_ge(T.sem[s], v)
        parts = []
        for (kind, a, b, rs), p, dst, m, final in tr:
            codes = kind == "c"
            if core == T.cores[p]:
                src = T.kq[:, a:b] if codes else T.kqs[:, a:b]
            else:
                src = T.rc[:, a:b] if codes else T.rp[:, a:b]
            if final:
                o = W * KO * (1 + R["slot"][p])
                out = T.mc[:, o + a:o + b] if codes else T.ms[:, o + a:o + b]
                sem = T.sem["arr%d" % R["slot"][p]]
            else:
                out = T.rc[:, a:b] if codes else T.rp[:, a:b]
                sem = T.sem[rs]
            if codes:
                src, out = src.bitcast(U8), out.bitcast(U8)
            rid, pid = topo.addr(dst, core)
            parts.append((out, src, sem, rid, pid, m))
            sent += count(m)
        if len(parts) == 1:
            out, src, sem, rid, pid, m = parts[0]
            g.remote_dma(out_ap=out, in_ap=src, remote_sem=sem, local_sem=T.sem.sent, pid=pid, routing_id=rid, dma_engine_mask=m)
        else:
            g.remote_dma_fused([RemoteDMATransfer(src=src, dst=out, dst_ids=[DstId(rid=rid, pnc=pid)], dma_engine_mask=m,
                                                  remote_sem=sem) for out, src, sem, rid, pid, m in parts], local_sem=T.sem.sent)
    if sent:
        g.wait_ge(T.sem.sent, sent)


def load_cache(g, T):
    g.sync.dma_start(T.mc[:, 0:2 * W].bitcast(U8), T.kc[:]).then_inc(T.sem.ld, 16)
    g.scalar.dma_start(T.ms[:, 0:2 * W], T.ks[:]).then_inc(T.sem.ld, 16)


def producer(g, T):
    load_cache(g, T)
    g.vector.memset(T.one[:], 1.0).then_inc(T.sem.ms0, 1)
    g.vector.memset(T.z[:], 0.0).then_inc(T.sem.ms0, 1)
    g.wait_ge(T.sem.ms0, 2)
    g.affine_select(T.z[:, 3:515:4], T.one[:], [[-1, W]], AluOpType.is_equal, 0.0, 0, 1).then_inc(T.sem.af, 1)
    g.vector.wait_ge(T.sem.af, 1)
    for b in range(4):
        g.vector.quantize_mx(T.sc[:, W * b:W * b + W], T.ss[:, W * b:W * b + W], T.z[:, 3 - b:515 - b]).then_inc(T.sem.sq, 1)
    g.tensor.wait_ge(T.sem.sq, 4)
    g.tensor.wait_ge(T.sem.ld, 32)
    for i in range(KO):
        for b in range(4):
            k = 4 * i + b
            g.tensor.matmul_mx(T.ps[:, 512 * k:512 * k + W], T.sc[:, W * b:W * b + W], T.ss[:, W * b:W * b + W],
                               T.mc[:, W * i:W * i + W], T.ms[:, W * i:W * i + W], True, True).then_inc(T.sem["mm%d" % k], 1)
    for i in range(KO):
        hh, qd = T.sem["hh%d" % i], T.sem["qd%d" % i]
        for b in range(4):
            k = 4 * i + b
            out, src = T.h[:, 512 * i + b:512 * i + 512:4], T.ps[:, 512 * k:512 * k + W]
            if b % 2:
                g.vector.wait_ge(T.sem["mm%d" % k], 1)
                g.vector.tensor_scalar(out, src, FACTOR, None, AluOpType.mult).then_inc(hh, 1)
            else:
                g.scalar.wait_ge(T.sem["mm%d" % k], 1)
                g.scalar.activation(out, src, ActivationFunctionType.Copy, scale=FACTOR).then_inc(hh, 1)
        g.vector.wait_ge(hh, 4)
        g.vector.quantize_mx(T.kq[:, W * i:W * i + W], T.kqs[:, W * i:W * i + W],
                             T.h[:, 512 * i:512 * i + 512]).then_inc(qd, 1)


def consumer(g, T, R, me):
    g.sync.dma_start(T.qb[:], T.q[:]).then_inc(T.sem.lq, 16)
    load_cache(g, T)
    g.vector.wait_ge(T.sem.lq, 16)
    g.vector.quantize_mx(T.qc[:], T.qs[:], T.qb[:]).then_inc(T.sem.qq, 1)
    g.tensor.wait_ge(T.sem.qq, 1)
    g.tensor.wait_ge(T.sem.ld, 32)
    own = T.tables["OWN"]
    mine = [p for p in R["slot"] if own[p] == me]
    order = [None] + [p for p in mine if p not in R["second"]] + [p for p in mine if p in R["second"]]
    bank = 0
    for j, p in enumerate(order):
        slot = 0 if p is None else 1 + R["slot"][p]
        if p is not None:
            g.tensor.wait_ge(T.sem["arr%d" % (slot - 1)], R["need"][p])
        o, cp = 2 * W * slot, T.sem["cp%d" % slot]
        n = 2 * W if j < 2 else W
        for k in range(2 * W // n):
            a, mo = o + k * n, T.sem["mo%d" % bank]
            src = T.ps[:, 512 * bank:512 * bank + n]
            g.tensor.matmul_mx(src, T.qc[:], T.qs[:], T.mc[:, a:a + n], T.ms[:, a:a + n], True, True).then_inc(mo, 1)
            if k == 0:
                g.vector.wait_ge(mo, 1)
                g.vector.tensor_copy(T.yo[:, a:a + n], src).then_inc(cp, 1)
            else:
                g.scalar.wait_ge(mo, 1)
                g.scalar.activation(T.yo[:, a:a + n], src, ActivationFunctionType.Copy).then_inc(cp, 1)
            bank += 1
        g.sync.wait_ge(cp, 2 * W // n)
        g.sync.dma_start(T.y[:, o:o + 2 * W], T.yo[:, o:o + 2 * W]).then_inc(T.sem.st, 16)
    g.sync.wait_ge(T.sem.st, 16 * len(order))


def rank_program(g, core, T, topo):
    R = roads(T, topo)
    rank = T.rank_of(core)
    if rank is not None:
        if T.tables["OWN"][rank] == rank:
            consumer(g, T, R, rank)
        else:
            producer(g, T)
    remote(g, core, T, topo, R)
